import numpy as np
import ml_dtypes


def mxq(x, axis, fmt="e4m3"):
    dtype, down = {"e4m3": (ml_dtypes.float8_e4m3fn, 7), "e5m2": (ml_dtypes.float8_e5m2, 14)}[fmt]
    v = np.moveaxis(np.asarray(x, np.float32).astype(ml_dtypes.bfloat16).astype(np.float64), axis, -1)
    blocks = v.reshape(v.shape[:-1] + (-1, 32))
    amax = np.abs(blocks).max(-1, keepdims=True)
    byte = np.maximum(np.where(amax > 0, np.frexp(amax)[1] - 1 + 127, 0) - down, 1)
    scale = np.exp2(byte - 127.0)
    codes = (blocks / scale).astype(np.float32).astype(dtype).astype(np.float64)
    return np.moveaxis((codes * scale).reshape(v.shape), -1, axis)


WIDE = False


def mx_kscale(k):
    if not WIDE:
        return np.ones(k)
    levels = np.array([10, -10, 5, -5, 0])
    if k % 512:
        return np.exp2(np.random.permutation(np.resize(levels, k // 32))).repeat(32)
    a = np.empty((k // 512, 16))
    for p in range(k // 512):
        a[p, :8] = np.random.permutation(np.resize(levels, 8))
        for g in range(8):
            far = levels[np.abs(levels - a[p, g]) >= 10]
            a[p, g + 8] = far[np.random.randint(len(far))]
    return np.exp2(a.ravel()).repeat(32)


def f64(x):
    return np.asarray(x).astype(np.float64)


def striped(idx):
    return np.tile(idx.reshape(-1, 16).T, (8, 1)).astype(np.uint16)


def unstriped(offs):
    return offs[:16].T.reshape(-1).astype(np.int64)


def striped8(idx):
    return np.concatenate([x.reshape(-1, 16).T for x in idx]).astype(np.uint16)


def runs(offs, k):
    lists = np.stack([offs[16 * r : 16 * r + 16].T.reshape(-1) for r in range(8)]).astype(np.int64)
    return lists[np.arange(k) % 512 // 64]


def pack_weight(w):
    k, n = w.shape
    w = f64(np.asarray(w, np.float32).astype(ml_dtypes.bfloat16)).reshape(k // 32, 32, n)
    amax = np.abs(w).max(1)
    byte = np.clip(np.where(amax > 0, np.frexp(amax)[1] - 1 + 127 - 7, 1), 1, 254)
    scaled = (w * np.exp2(127.0 - byte)[:, None, :]).reshape(k, n).astype(np.float32)
    words = np.ascontiguousarray(scaled.reshape(k // 512, 128, 4, n).transpose(0, 1, 3, 2)).astype(ml_dtypes.float8_e4m3fn).view(np.uint8)
    return words, np.ascontiguousarray(byte.astype(np.uint8).reshape(k // 512, 16, n))


def unpack_weight(words, scales):
    g, p, n, _ = words.shape
    vals = np.ascontiguousarray(words).view(ml_dtypes.float8_e4m3fn).astype(np.float64) * np.repeat(np.exp2(scales.astype(np.float64) - 127.0), 8, axis=1)[..., None]
    return vals.transpose(0, 1, 3, 2).reshape(g * 512, n)


E2M1 = np.array([0.0, 0.5, 1.0, 1.5, 2.0, 3.0, 4.0, 6.0, -0.0, -0.5, -1.0, -1.5, -2.0, -3.0, -4.0, -6.0])


def pack_fp4(w):
    k, n = w.shape
    w = f64(np.asarray(w, np.float32).astype(ml_dtypes.bfloat16)).reshape(k // 32, 32, n)
    amax = np.abs(w).max(1)
    mant, ex = np.frexp(amax / 6.0)
    byte = np.clip(np.where(amax > 0, np.where(mant > 0.5, ex, ex - 1) + 127, 1), 1, 254)
    scaled = (w * np.exp2(127.0 - byte)[:, None, :]).reshape(k, n).astype(np.float32)
    c = np.ascontiguousarray(scaled.reshape(k // 512, 128, 4, n).transpose(0, 1, 3, 2)).astype(ml_dtypes.float4_e2m1fn).view(np.uint8) & 0xF
    words = (c[..., 0::2] | (c[..., 1::2] << 4)).reshape(k // 512, 128, 2 * n)
    return np.ascontiguousarray(words), np.ascontiguousarray(byte.astype(np.uint8).reshape(k // 512, 16, n))


def unpack_fp4(words, scales):
    g, _, n = scales.shape
    words = np.ascontiguousarray(words).reshape(g, 128, n, 2)
    nib = np.empty((g, 128, n, 4), np.uint8)
    nib[..., 0::2] = words & 0xF
    nib[..., 1::2] = words >> 4
    vals = E2M1[nib] * np.repeat(np.exp2(scales.astype(np.float64) - 127.0), 8, axis=1)[..., None]
    return vals.transpose(0, 1, 3, 2).reshape(g * 512, n)


K, T, S, H, W, G = 512, 2048, 256, 512, 128, 2048


def setup_inputs():
    n = np.random.standard_normal
    s = mx_kscale(K)[:, None]
    packed_xT = pack_weight(n((K, T)) * s)
    packed_w1 = pack_fp4(n((K, H)) / np.sqrt(K) / s)
    packed_dT = pack_weight(n((K, G)) / s)
    perm = np.random.permutation(S)
    return {
        "x_words": packed_xT[0],
        "x_scales": packed_xT[1],
        "w1_words": packed_w1[0],
        "w1_scales": packed_w1[1],
        "gs": (np.random.uniform(0.5, 1.5, (K, 1)) * s).astype(np.float32),
        "d_words": packed_dT[0],
        "d_scales": packed_dT[1],
        "offs": striped(np.random.permutation(T)[:S]),
        "n1": striped(perm[:W]),
        "n2": striped(perm[W:]),
        "n3": striped(np.random.permutation(S)),
        "k1": striped8(np.random.randint(0, G, (8, H))),
        "n4": striped8(np.stack([np.random.permutation(S) for _ in range(8)])),
    }


def reference(x_words, x_scales, w1_words, w1_scales, gs, d_words, d_scales, offs, n1, n2, n3, k1, n4):
    d_k1 = unpack_weight(d_words, d_scales)[np.arange(K)[:, None], runs(k1, K)]
    xq = unpack_weight(x_words, x_scales)[:, unstriped(offs)]
    y = unpack_fp4(w1_words, w1_scales).T @ xq
    pa = y[:, unstriped(n1)]
    pb = y[:, unstriped(n2)]
    rb = np.minimum(pa, pb)
    ra = np.maximum(pa, pb)
    ds = np.zeros((H, S))
    ds[:, unstriped(n1)] = ra
    dt = ds.copy()
    dt[:, unstriped(n2)] = rb
    z = f64(gs) * (dt - dt[:, unstriped(n3)])
    h = 0.0625 * ((d_k1.T @ mxq(z, 0, "e4m3")))
    return h / (np.abs(h[np.arange(H)[:, None], runs(n4, H)]) + 0.5)

@@ -1,0 +1,218 @@
+from contextlib import ExitStack
+
+import concourse.mybir as mybir
+
+K, T, S, H, W, G = 512, 2048, 256, 512, 128, 2048
+FLOPS = 2 * K * H * S + 2 * H * K * S
+
+F32 = mybir.dt.float32
+BF16 = mybir.dt.bfloat16
+I32 = mybir.dt.int32
+U32 = mybir.dt.uint32
+U16 = mybir.dt.uint16
+U8 = mybir.dt.uint8
+FP8X4 = mybir.dt.float8_e4m3fn_x4
+FP4X4 = mybir.dt.float4_e2m1fn_x4
+ALU = mybir.AluOpType
+ACT = mybir.ActivationFunctionType
+
+P = 128
+PACK = 4
+HALF = S // 2
+
+
+def tile_picked_denseorddnorm_none_p_kernel(
+    tc, x_words, x_scales, w1_words, w1_scales, gs, d_words, d_scales, offs, n1, n2, n3, k1, n4, out
+):
+    nc = tc.nc
+    with ExitStack() as ctx:
+        lists = ctx.enter_context(tc.tile_pool(name="lists", bufs=1))
+        sb = ctx.enter_context(tc.tile_pool(name="sb", bufs=1))
+        ps = ctx.enter_context(tc.psum_pool(name="ps", bufs=1))
+
+        def load_list(src, name):
+            tile = lists.tile([P, src.shape[1]], U16, name=name)
+            nc.sync.dma_start(tile[:], src)
+            return tile
+
+        def word_view(words):
+            return words[0].rearrange("p n r -> p (n r)").bitcast(I32)
+
+        xs_tab = sb.tile([P, T], U8, name="xs_tab")
+        nc.vector.memset(xs_tab[:].bitcast(I32), 0)
+        ws_raw = sb.tile([P, H], U8, name="ws_raw")
+        nc.vector.memset(ws_raw[:].bitcast(I32), 0)
+        ds_tab = sb.tile([P, G], U8, name="ds_tab")
+        nc.vector.memset(ds_tab[:].bitcast(I32), 0)
+        ds_plane = sb.tile([P, H], U8, name="ds_plane", align_bytes=64)
+        nc.vector.memset(ds_plane[:].bitcast(I32), 0)
+        eight = sb.tile([P, 1], F32, name="eight")
+        nc.vector.memset(eight[:], 8.0)
+
+        offs_t = load_list(offs, "offs_t")
+        ww_raw = sb.tile([P, 2 * H], U8, name="ww_raw")
+        nc.sync.dma_start(ww_raw[:].bitcast(I32), w1_words[0].bitcast(I32))
+        xw_tab = sb.tile([P, T], U32, name="xw_tab")
+        nc.sync.dma_start(xw_tab[:].bitcast(I32), word_view(x_words))
+        for q in range(4):
+            nc.scalar.dma_start(xs_tab[32 * q : 32 * q + 4, :].bitcast(I32), x_scales[0, 4 * q : 4 * q + 4, :].bitcast(I32))
+        for q in range(4):
+            nc.scalar.dma_start(ws_raw[32 * q : 32 * q + 4, :].bitcast(I32), w1_scales[0, 4 * q : 4 * q + 4, :].bitcast(I32))
+        n1_t = load_list(n1, "n1_t")
+        n2_t = load_list(n2, "n2_t")
+
+        k1_t = load_list(k1, "k1_t")
+        dw_tab = sb.tile([P, G], U32, name="dw_tab")
+        nc.sync.dma_start(ds_tab[0:P:8, :].bitcast(I32), d_scales[0].bitcast(I32))
+        nc.sync.dma_start(dw_tab[:].bitcast(I32), word_view(d_words))
+        gain = sb.tile([P, PACK], F32, name="gain")
+        nc.sync.dma_start(gain[:], gs.rearrange("(p t) o -> p (t o)", t=PACK))
+        n3_t = load_list(n3, "n3_t")
+        n4_t = load_list(n4, "n4_t")
+
+        roots = [sb.tile([P, S], F32, name="root%d" % t) for t in range(PACK)]
+
+        ww = sb.tile([P, 2 * H], U8, name="ww", align_bytes=64)
+        nc.vector.tensor_copy(
+            ww[:].rearrange("p (t m b) -> p t m b", t=PACK, b=2),
+            ww_raw[:].rearrange("p (m t b) -> p t m b", t=PACK, b=2),
+        )
+        xs = sb.tile([P, S], U8, name="xs", align_bytes=64)
+        nc.vector.tensor_copy(xs[:], xs_tab[:].indirect(offs_t[:]))
+        ws = sb.tile([P, H], U8, name="ws", align_bytes=64)
+        nc.vector.tensor_copy(
+            ws[:].rearrange("p (t m) -> p t m", t=PACK), ws_raw[:].rearrange("p (m t) -> p t m", t=PACK)
+        )
+        xw = sb.tile([P, S], U32, name="xw", align_bytes=64)
+        nc.vector.tensor_copy(xw[:], xw_tab[:].indirect(offs_t[:]))
+
+        y = []
+        for t in range(PACK):
+            y_ps = ps.tile([P, S], F32, name="y_ps%d" % t, tag="bank%d" % t)
+            nc.tensor.matmul_mx(
+                out=y_ps[:],
+                lhsT=ww[:, 2 * P * t : 2 * P * (t + 1)].bitcast(FP4X4),
+                lhsT_scale=ws[:, P * t : P * (t + 1)],
+                rhs=xw[:].bitcast(FP8X4),
+                rhs_scale=xs[:],
+                start=True,
+                stop=True,
+            )
+            y_t = sb.tile([P, S], F32, name="y%d" % t)
+            nc.vector.tensor_copy(y_t[:], y_ps[:])
+            y.append(y_t)
+
+        larger, smaller, dt = [], [], []
+
+        def fetch_pairs(t):
+            pa = sb.tile([P, W], F32, name="pa%d" % t)
+            pb = sb.tile([P, W], F32, name="pb%d" % t)
+            nc.scalar.activation(pa[:], y[t][:].indirect(n1_t[:]), ACT.Copy)
+            nc.scalar.activation(pb[:], y[t][:].indirect(n2_t[:]), ACT.Copy)
+            ra = sb.tile([P, W], F32, name="ra%d" % t)
+            rb = sb.tile([P, W], F32, name="rb%d" % t)
+            nc.vector.tensor_tensor(ra[:], pa[:], pb[:], ALU.max)
+            nc.vector.tensor_tensor(rb[:], pa[:], pb[:], ALU.min)
+            larger.append(ra)
+            smaller.append(rb)
+            dt.append(sb.tile([P, S], F32, name="dt%d" % t))
+
+        def put_larger(t):
+            nc.scalar.activation(dt[t][:].indirect(n1_t[:]), larger[t][:], ACT.Copy)
+
+        def put_smaller(t):
+            nc.scalar.activation(dt[t][:].indirect(n2_t[:]), smaller[t][:], ACT.Copy)
+            nc.vector.tensor_scalar(dts[:, t, :], dt[t][:], gain[:, t : t + 1], None, ALU.mult)
+
+        for t in range(PACK):
+            fetch_pairs(t)
+
+        dw_g = sb.tile([P, H], U32, name="dw_g", tag="dw_g_then_dts")
+        ds_g = sb.tile([P, H], U8, name="ds_g")
+        for u in range(2):
+            cols = slice(u * H // 2, (u + 1) * H // 2)
+            entries = k1_t[:, u * H // 32 : (u + 1) * H // 32]
+            nc.vector.tensor_copy(ds_g[:, cols], ds_tab[:].indirect(entries))
+        ds_d = sb.tile([P, H], U8, name="ds_d")
+        nc.vector.tensor_copy(
+            ds_d[:].rearrange("p (t m) -> p t m", t=PACK), ds_g[:].rearrange("p (m t) -> p t m", t=PACK)
+        )
+        for q in range(4):
+            nc.sync.dma_start(
+                ds_plane[32 * q : 32 * q + 4, :].bitcast(I32), ds_d[32 * q : 32 * q + 32 : 8, :].bitcast(I32)
+            )
+        for u in range(2):
+            cols = slice(u * H // 2, (u + 1) * H // 2)
+            entries = k1_t[:, u * H // 32 : (u + 1) * H // 32]
+            nc.vector.tensor_copy(dw_g[:, cols], dw_tab[:].indirect(entries))
+        dw = sb.tile([P, H], U32, name="dw", align_bytes=64)
+        nc.vector.tensor_copy(
+            dw[:].rearrange("p (t m) -> p t m", t=PACK), dw_g[:].rearrange("p (m t) -> p t m", t=PACK)
+        )
+
+        dts = sb.tile([P, PACK, S], F32, name="dts", tag="dw_g_then_dts")
+        for t0 in (0, 2):
+            put_larger(t0)
+            put_larger(t0 + 1)
+            put_smaller(t0)
+            put_smaller(t0 + 1)
+
+        sums = []
+        for u in range(2):
+            cols = slice(u * HALF, (u + 1) * HALF)
+            other = sb.tile([P, PACK, HALF], F32, name="other%d" % u)
+            for t in range(PACK):
+                nc.scalar.activation(
+                    other[:, t, :], dts[:, t, :].indirect(n3_t[:, u * HALF // 16 : (u + 1) * HALF // 16]), ACT.Copy
+                )
+            z = sb.tile([P, HALF * PACK], BF16, name="z%d" % u, align_bytes=64)
+            nc.vector.tensor_tensor(
+                z[:].rearrange("p (c i t) -> p c t i", i=4, t=PACK),
+                dts[:, :, cols].rearrange("p t (c i) -> p c t i", i=4),
+                other[:].rearrange("p t (c i) -> p c t i", i=4),
+                ALU.subtract,
+            )
+            zw = sb.tile([P, HALF], U32, name="zw%d" % u, align_bytes=64)
+            zs = sb.tile([P, HALF], U8, name="zs%d" % u, align_bytes=64)
+            nc.vector.quantize_mx(out=zw[:].bitcast(FP8X4), scales=zs[:], in_=z[:])
+            row = []
+            for t in range(PACK):
+                h_ps = ps.tile([P, HALF], F32, name="h_ps%d_%d" % (u, t), tag="bank%d" % (PACK * (1 - u) + t))
+                nc.tensor.matmul_mx(
+                    out=h_ps[:],
+                    lhsT=dw[:, P * t : P * (t + 1)].bitcast(FP8X4),
+                    lhsT_scale=ds_plane[:, P * t : P * (t + 1)],
+                    rhs=zw[:].bitcast(FP8X4),
+                    rhs_scale=zs[:],
+                    start=True,
+                    stop=True,
+                )
+                row.append(h_ps)
+            sums.append(row)
+
+        def root(u, t, size):
+            nc.scalar.activation(
+                roots[t][:, u * HALF : (u + 1) * HALF], size[:], ACT.Abs_reciprocal_sqrt, bias=eight[:], scale=1.0
+            )
+
+        for t in range(PACK):
+            size = sb.tile([P, HALF], F32, name="size0_%d" % t)
+            nc.scalar.activation(size[:], sums[0][t][:], ACT.Abs)
+            root(0, t, size)
+        out_rows = out.rearrange("(p t) n -> p t n", t=PACK)
+        for t in range(PACK):
+            size = sb.tile([P, HALF], F32, name="size1_%d" % t)
+            negated = sb.tile([P, HALF], F32, name="negated%d" % t)
+            nc.vector.tensor_scalar(negated[:], sums[1][t][:], -1.0, None, ALU.mult)
+            nc.vector.tensor_tensor(size[:], sums[1][t][:], negated[:], ALU.max)
+            root(1, t, size)
+            fetched = sb.tile([P, S], F32, name="fetched%d" % t)
+            part = sb.tile([P, S], F32, name="part%d" % t)
+            for u in range(2):
+                cols = slice(u * HALF, (u + 1) * HALF)
+                entries = n4_t[:, u * HALF // 16 : (u + 1) * HALF // 16]
+                nc.scalar.activation(fetched[:, cols], roots[t][:].indirect(entries), ACT.Copy)
+                nc.vector.tensor_tensor(part[:, cols], sums[u][t][:], fetched[:, cols], ALU.mult)
+            result = sb.tile([P, S], F32, name="result%d" % t)
+            nc.vector.tensor_tensor(result[:], part[:], fetched[:], ALU.mult)
+            nc.sync.dma_start(out_rows[:, t, :], result[:])

@@ -41,7 +41,7 @@ def tile_picked_denseorddnorm_none_p_kernel(
         xs_tab = sb.tile([P, T], U8, name="xs_tab")
         nc.vector.memset(xs_tab[:].bitcast(I32), 0)
         ws_raw = sb.tile([P, H], U8, name="ws_raw")
-        nc.vector.memset(ws_raw[:].bitcast(I32), 0)
+        nc.gpsimd.memset(ws_raw[:].bitcast(I32), 0)
         ds_tab = sb.tile([P, G], U8, name="ds_tab")
         nc.vector.memset(ds_tab[:].bitcast(I32), 0)
         ds_plane = sb.tile([P, H], U8, name="ds_plane", align_bytes=64)
@@ -49,15 +49,18 @@ def tile_picked_denseorddnorm_none_p_kernel(
         eight = sb.tile([P, 1], F32, name="eight")
         nc.vector.memset(eight[:], 8.0)
 
+        def load_scale_rows(engine, tile, rows, q):
+            engine.dma_start(tile[32 * q : 32 * q + 4, :].bitcast(I32), rows[0, 4 * q : 4 * q + 4, :].bitcast(I32))
+
         offs_t = load_list(offs, "offs_t")
+        xw_tab = sb.tile([P, T], U32, name="xw_tab")
+        nc.scalar.dma_start(xw_tab[:].bitcast(I32), word_view(x_words))
         ww_raw = sb.tile([P, 2 * H], U8, name="ww_raw")
         nc.sync.dma_start(ww_raw[:].bitcast(I32), w1_words[0].bitcast(I32))
-        xw_tab = sb.tile([P, T], U32, name="xw_tab")
-        nc.sync.dma_start(xw_tab[:].bitcast(I32), word_view(x_words))
         for q in range(4):
-            nc.scalar.dma_start(xs_tab[32 * q : 32 * q + 4, :].bitcast(I32), x_scales[0, 4 * q : 4 * q + 4, :].bitcast(I32))
+            load_scale_rows(nc.sync, xs_tab, x_scales, q)
         for q in range(4):
-            nc.scalar.dma_start(ws_raw[32 * q : 32 * q + 4, :].bitcast(I32), w1_scales[0, 4 * q : 4 * q + 4, :].bitcast(I32))
+            load_scale_rows(nc.sync if q < 2 else nc.gpsimd, ws_raw, w1_scales, q)
         n1_t = load_list(n1, "n1_t")
         n2_t = load_list(n2, "n2_t")
 
@@ -72,10 +75,13 @@ def tile_picked_denseorddnorm_none_p_kernel(
 
         roots = [sb.tile([P, S], F32, name="root%d" % t) for t in range(PACK)]
 
+        warm = sb.tile([P, 1], F32, name="warm")
+        nc.scalar.activation(warm[:], eight[:], ACT.Abs_reciprocal_sqrt, bias=eight[:], scale=1.0)
+
         ww = sb.tile([P, 2 * H], U8, name="ww", align_bytes=64)
-        nc.vector.tensor_copy(
-            ww[:].rearrange("p (t m b) -> p t m b", t=PACK, b=2),
-            ww_raw[:].rearrange("p (m t b) -> p t m b", t=PACK, b=2),
+        nc.scalar.copy(
+            ww[:].bitcast(U16).rearrange("p (t m) -> p t m", t=PACK),
+            ww_raw[:].bitcast(U16).rearrange("p (m t) -> p t m", t=PACK),
         )
         xs = sb.tile([P, S], U8, name="xs", align_bytes=64)
         nc.vector.tensor_copy(xs[:], xs_tab[:].indirect(offs_t[:]))
@@ -84,23 +90,32 @@ def tile_picked_denseorddnorm_none_p_kernel(
             ws[:].rearrange("p (t m) -> p t m", t=PACK), ws_raw[:].rearrange("p (m t) -> p t m", t=PACK)
         )
         xw = sb.tile([P, S], U32, name="xw", align_bytes=64)
-        nc.vector.tensor_copy(xw[:], xw_tab[:].indirect(offs_t[:]))
+        halves = [slice(u * HALF, (u + 1) * HALF) for u in range(2)]
 
-        y = []
-        for t in range(PACK):
-            y_ps = ps.tile([P, S], F32, name="y_ps%d" % t, tag="bank%d" % t)
+        def half_of(offsets, u):
+            return offsets[:, u * HALF // 16 : (u + 1) * HALF // 16]
+
+        for u in range(2):
+            nc.vector.tensor_copy(xw[:, halves[u]], xw_tab[:].indirect(half_of(offs_t, u)))
+
+        def first_product(t, cols, bank):
+            y_ps = ps.tile([P, cols.stop - cols.start], F32, name="y_ps%d" % bank, tag="bank%d" % bank)
             nc.tensor.matmul_mx(
                 out=y_ps[:],
                 lhsT=ww[:, 2 * P * t : 2 * P * (t + 1)].bitcast(FP4X4),
                 lhsT_scale=ws[:, P * t : P * (t + 1)],
-                rhs=xw[:].bitcast(FP8X4),
-                rhs_scale=xs[:],
+                rhs=xw[:, cols].bitcast(FP8X4),
+                rhs_scale=xs[:, cols],
                 start=True,
                 stop=True,
             )
-            y_t = sb.tile([P, S], F32, name="y%d" % t)
-            nc.vector.tensor_copy(y_t[:], y_ps[:])
-            y.append(y_t)
+            return y_ps
+
+        y = [sb.tile([P, S], F32, name="y%d" % t) for t in range(PACK)]
+        for u in range(2):
+            nc.scalar.copy(y[0][:, halves[u]], first_product(0, halves[u], PACK * u)[:])
+        for t in range(1, PACK):
+            nc.vector.tensor_copy(y[t][:], first_product(t, slice(0, S), t)[:])
 
         larger, smaller, dt = [], [], []
 
@@ -165,7 +180,7 @@ def tile_picked_denseorddnorm_none_p_kernel(
                 nc.scalar.activation(
                     other[:, t, :], dts[:, t, :].indirect(n3_t[:, u * HALF // 16 : (u + 1) * HALF // 16]), ACT.Copy
                 )
-            z = sb.tile([P, HALF * PACK], BF16, name="z%d" % u, align_bytes=64)
+            z = sb.tile([P, HALF * PACK], BF16, name="z%d" % u, tag="z", align_bytes=64)
             nc.vector.tensor_tensor(
                 z[:].rearrange("p (c i t) -> p c t i", i=4, t=PACK),
                 dts[:, :, cols].rearrange("p t (c i) -> p c t i", i=4),
@@ -190,29 +205,56 @@ def tile_picked_denseorddnorm_none_p_kernel(
                 row.append(h_ps)
             sums.append(row)
 
-        def root(u, t, size):
-            nc.scalar.activation(
-                roots[t][:, u * HALF : (u + 1) * HALF], size[:], ACT.Abs_reciprocal_sqrt, bias=eight[:], scale=1.0
-            )
+        early, late = (0, 1), (2, 3)
+        late_roots = {t: sb.tile([P, S], F32, name="late_root%d" % t) for t in late}
 
+        def size_on_scalar(u, t):
+            size = sb.tile([P, HALF], F32, name="size%d_%d" % (u, t))
+            nc.scalar.activation(size[:], sums[u][t][:], ACT.Abs)
+            return size
+
+        def size_on_vector(u, t):
+            size = sb.tile([P, HALF], F32, name="size%d_%d" % (u, t))
+            negated = sb.tile([P, HALF], F32, name="negated%d_%d" % (u, t))
+            nc.vector.tensor_scalar(negated[:], sums[u][t][:], -1.0, None, ALU.mult)
+            nc.vector.tensor_tensor(size[:], sums[u][t][:], negated[:], ALU.max)
+            return size
+
+        def root(u, t, size):
+            dst = roots[t] if t in early else late_roots[t]
+            nc.scalar.activation(dst[:, halves[u]], size[:], ACT.Abs_reciprocal_sqrt, bias=eight[:], scale=1.0)
+
+        sizes = [size_on_scalar(0, t) for t in range(PACK)]
         for t in range(PACK):
-            size = sb.tile([P, HALF], F32, name="size0_%d" % t)
-            nc.scalar.activation(size[:], sums[0][t][:], ACT.Abs)
-            root(0, t, size)
+            root(0, t, sizes[t])
+        sizes = [size_on_scalar(1, t) for t in early] + [size_on_vector(1, t) for t in late]
         out_rows = out.rearrange("(p t) n -> p t n", t=PACK)
-        for t in range(PACK):
-            size = sb.tile([P, HALF], F32, name="size1_%d" % t)
-            negated = sb.tile([P, HALF], F32, name="negated%d" % t)
-            nc.vector.tensor_scalar(negated[:], sums[1][t][:], -1.0, None, ALU.mult)
-            nc.vector.tensor_tensor(size[:], sums[1][t][:], negated[:], ALU.max)
-            root(1, t, size)
+
+        def fetch(t):
             fetched = sb.tile([P, S], F32, name="fetched%d" % t)
-            part = sb.tile([P, S], F32, name="part%d" % t)
             for u in range(2):
-                cols = slice(u * HALF, (u + 1) * HALF)
                 entries = n4_t[:, u * HALF // 16 : (u + 1) * HALF // 16]
-                nc.scalar.activation(fetched[:, cols], roots[t][:].indirect(entries), ACT.Copy)
-                nc.vector.tensor_tensor(part[:, cols], sums[u][t][:], fetched[:, cols], ALU.mult)
+                nc.scalar.activation(fetched[:, halves[u]], roots[t][:].indirect(entries), ACT.Copy)
+            return fetched
+
+        def times_sums(t, factor, name):
+            product = sb.tile([P, S], F32, name=name)
+            for u in range(2):
+                nc.vector.tensor_tensor(product[:, halves[u]], sums[u][t][:], factor[:, halves[u]], ALU.mult)
+            return product
+
+        for t in early:
+            root(1, t, sizes[t])
+        fetched = {early[0]: fetch(early[0])}
+        for t in late:
+            root(1, t, sizes[t])
+            nc.vector.tensor_tensor(roots[t][:], late_roots[t][:], late_roots[t][:], ALU.mult)
+        fetched[early[1]] = fetch(early[1])
+        for t in early:
+            part = times_sums(t, fetched[t], "part%d" % t)
             result = sb.tile([P, S], F32, name="result%d" % t)
-            nc.vector.tensor_tensor(result[:], part[:], fetched[:], ALU.mult)
+            nc.vector.tensor_tensor(result[:], part[:], fetched[t][:], ALU.mult)
+            nc.sync.dma_start(out_rows[:, t, :], result[:])
+        for t in late:
+            result = times_sums(t, fetch(t), "result%d" % t)
             nc.sync.dma_start(out_rows[:, t, :], result[:])

@@ -53,15 +53,15 @@ def tile_picked_denseorddnorm_none_p_kernel(
             engine.dma_start(tile[32 * q : 32 * q + 4, :].bitcast(I32), rows[0, 4 * q : 4 * q + 4, :].bitcast(I32))
 
         offs_t = load_list(offs, "offs_t")
+        ww_raw = sb.tile([P, 2 * H], U8, name="ww_raw")
+        nc.scalar.dma_start(ww_raw[:].bitcast(I32), w1_words[0].bitcast(I32))
+        n1_t = load_list(n1, "n1_t")
         xw_tab = sb.tile([P, T], U32, name="xw_tab")
         nc.scalar.dma_start(xw_tab[:].bitcast(I32), word_view(x_words))
-        ww_raw = sb.tile([P, 2 * H], U8, name="ww_raw")
-        nc.sync.dma_start(ww_raw[:].bitcast(I32), w1_words[0].bitcast(I32))
         for q in range(4):
             load_scale_rows(nc.sync, xs_tab, x_scales, q)
         for q in range(4):
             load_scale_rows(nc.sync if q < 2 else nc.gpsimd, ws_raw, w1_scales, q)
-        n1_t = load_list(n1, "n1_t")
         n2_t = load_list(n2, "n2_t")
 
         k1_t = load_list(k1, "k1_t")
@@ -86,9 +86,10 @@ def tile_picked_denseorddnorm_none_p_kernel(
         xs = sb.tile([P, S], U8, name="xs", align_bytes=64)
         nc.vector.tensor_copy(xs[:], xs_tab[:].indirect(offs_t[:]))
         ws = sb.tile([P, H], U8, name="ws", align_bytes=64)
-        nc.vector.tensor_copy(
-            ws[:].rearrange("p (t m) -> p t m", t=PACK), ws_raw[:].rearrange("p (m t) -> p t m", t=PACK)
-        )
+        ws_dealt = ws[:].rearrange("p (t m) -> p t m", t=PACK)
+        ws_given = ws_raw[:].rearrange("p (m t) -> p t m", t=PACK)
+        nc.vector.tensor_copy(ws_dealt[:, :1, :], ws_given[:, :1, :])
+        nc.vector.tensor_copy(ws_dealt[:, 1:, :], ws_given[:, 1:, :])
         xw = sb.tile([P, S], U32, name="xw", align_bytes=64)
         halves = [slice(u * HALF, (u + 1) * HALF) for u in range(2)]
 
@@ -191,70 +192,43 @@ def tile_picked_denseorddnorm_none_p_kernel(
             zs = sb.tile([P, HALF], U8, name="zs%d" % u, align_bytes=64)
             nc.vector.quantize_mx(out=zw[:].bitcast(FP8X4), scales=zs[:], in_=z[:])
             row = []
-            for t in range(PACK):
-                h_ps = ps.tile([P, HALF], F32, name="h_ps%d_%d" % (u, t), tag="bank%d" % (PACK * (1 - u) + t))
-                nc.tensor.matmul_mx(
-                    out=h_ps[:],
-                    lhsT=dw[:, P * t : P * (t + 1)].bitcast(FP8X4),
-                    lhsT_scale=ds_plane[:, P * t : P * (t + 1)],
-                    rhs=zw[:].bitcast(FP8X4),
-                    rhs_scale=zs[:],
-                    start=True,
-                    stop=True,
-                )
+            for v in range(2):
+                h_ps = ps.tile([P, 2, HALF], F32, name="h_ps%d_%d" % (u, v), tag="bank%d" % (PACK + 1 - 5 * u + v))
+                for w in range(2):
+                    t = 2 * v + w
+                    nc.tensor.matmul_mx(
+                        out=h_ps[:, w, :],
+                        lhsT=dw[:, P * t : P * (t + 1)].bitcast(FP8X4),
+                        lhsT_scale=ds_plane[:, P * t : P * (t + 1)],
+                        rhs=zw[:].bitcast(FP8X4),
+                        rhs_scale=zs[:],
+                        start=True,
+                        stop=True,
+                    )
                 row.append(h_ps)
             sums.append(row)
 
-        early, late = (0, 1), (2, 3)
-        late_roots = {t: sb.tile([P, S], F32, name="late_root%d" % t) for t in late}
+        late_roots = sb.tile([P, PACK - 1, S], F32, name="late_roots")
+        for u in range(2):
+            size = sb.tile([P, PACK, HALF], F32, name="size%d" % u)
+            for v in range(2):
+                nc.scalar.activation(size[:, 2 * v : 2 * v + 2, :], sums[u][v][:], ACT.Abs)
+            for dst, src in ((roots[0][:, halves[u]], size[:, 0, :]), (late_roots[:, :, halves[u]], size[:, 1:, :])):
+                nc.scalar.activation(dst, src, ACT.Abs_reciprocal_sqrt, bias=eight[:], scale=1.0)
+        for t in range(1, PACK):
+            nc.vector.tensor_tensor(roots[t][:], late_roots[:, t - 1, :], late_roots[:, t - 1, :], ALU.mult)
 
-        def size_on_scalar(u, t):
-            size = sb.tile([P, HALF], F32, name="size%d_%d" % (u, t))
-            nc.scalar.activation(size[:], sums[u][t][:], ACT.Abs)
-            return size
-
-        def size_on_vector(u, t):
-            size = sb.tile([P, HALF], F32, name="size%d_%d" % (u, t))
-            negated = sb.tile([P, HALF], F32, name="negated%d_%d" % (u, t))
-            nc.vector.tensor_scalar(negated[:], sums[u][t][:], -1.0, None, ALU.mult)
-            nc.vector.tensor_tensor(size[:], sums[u][t][:], negated[:], ALU.max)
-            return size
-
-        def root(u, t, size):
-            dst = roots[t] if t in early else late_roots[t]
-            nc.scalar.activation(dst[:, halves[u]], size[:], ACT.Abs_reciprocal_sqrt, bias=eight[:], scale=1.0)
-
-        sizes = [size_on_scalar(0, t) for t in range(PACK)]
-        for t in range(PACK):
-            root(0, t, sizes[t])
-        sizes = [size_on_scalar(1, t) for t in early] + [size_on_vector(1, t) for t in late]
         out_rows = out.rearrange("(p t) n -> p t n", t=PACK)
-
-        def fetch(t):
+        for t in range(PACK):
             fetched = sb.tile([P, S], F32, name="fetched%d" % t)
-            for u in range(2):
-                entries = n4_t[:, u * HALF // 16 : (u + 1) * HALF // 16]
-                nc.scalar.activation(fetched[:, halves[u]], roots[t][:].indirect(entries), ACT.Copy)
-            return fetched
-
-        def times_sums(t, factor, name):
-            product = sb.tile([P, S], F32, name=name)
-            for u in range(2):
-                nc.vector.tensor_tensor(product[:, halves[u]], sums[u][t][:], factor[:, halves[u]], ALU.mult)
-            return product
-
-        for t in early:
-            root(1, t, sizes[t])
-        fetched = {early[0]: fetch(early[0])}
-        for t in late:
-            root(1, t, sizes[t])
-            nc.vector.tensor_tensor(roots[t][:], late_roots[t][:], late_roots[t][:], ALU.mult)
-        fetched[early[1]] = fetch(early[1])
-        for t in early:
-            part = times_sums(t, fetched[t], "part%d" % t)
             result = sb.tile([P, S], F32, name="result%d" % t)
-            nc.vector.tensor_tensor(result[:], part[:], fetched[t][:], ALU.mult)
-            nc.sync.dma_start(out_rows[:, t, :], result[:])
-        for t in late:
-            result = times_sums(t, fetch(t), "result%d" % t)
+            for u in range(2):
+                nc.scalar.activation(fetched[:, halves[u]], roots[t][:].indirect(half_of(n4_t, u)), ACT.Copy)
+                nc.vector.tensor_tensor(
+                    result[:, halves[u]], sums[u][t // 2][:, t % 2, :], fetched[:, halves[u]], ALU.mult
+                )
+            if t == 0:
+                part = result
+                result = sb.tile([P, S], F32, name="result0_whole")
+                nc.vector.tensor_tensor(result[:], part[:], fetched[:], ALU.mult)
             nc.sync.dma_start(out_rows[:, t, :], result[:])

from contextlib import ExitStack

import concourse.mybir as mybir

K, T, S, H, W, G = 512, 2048, 256, 512, 128, 2048
FLOPS = 2 * K * H * S + 2 * H * K * S

F32 = mybir.dt.float32
BF16 = mybir.dt.bfloat16
I32 = mybir.dt.int32
U32 = mybir.dt.uint32
U16 = mybir.dt.uint16
U8 = mybir.dt.uint8
FP8X4 = mybir.dt.float8_e4m3fn_x4
FP4X4 = mybir.dt.float4_e2m1fn_x4
ALU = mybir.AluOpType
ACT = mybir.ActivationFunctionType

P = 128
PACK = 4
HALF = S // 2


def tile_picked_denseorddnorm_none_p_kernel(
    tc, x_words, x_scales, w1_words, w1_scales, gs, d_words, d_scales, offs, n1, n2, n3, k1, n4, out
):
    nc = tc.nc
    with ExitStack() as ctx:
        lists = ctx.enter_context(tc.tile_pool(name="lists", bufs=1))
        sb = ctx.enter_context(tc.tile_pool(name="sb", bufs=1))
        ps = ctx.enter_context(tc.psum_pool(name="ps", bufs=1))

        def load_list(src, name):
            tile = lists.tile([P, src.shape[1]], U16, name=name)
            nc.sync.dma_start(tile[:], src)
            return tile

        def word_view(words):
            return words[0].rearrange("p n r -> p (n r)").bitcast(I32)

        xs_tab = sb.tile([P, T], U8, name="xs_tab")
        nc.vector.memset(xs_tab[:].bitcast(I32), 0)
        ws_raw = sb.tile([P, H], U8, name="ws_raw")
        nc.gpsimd.memset(ws_raw[:].bitcast(I32), 0)
        ds_tab = sb.tile([P, G], U8, name="ds_tab")
        nc.vector.memset(ds_tab[:].bitcast(I32), 0)
        ds_plane = sb.tile([P, H], U8, name="ds_plane", align_bytes=64)
        nc.vector.memset(ds_plane[:].bitcast(I32), 0)
        eight = sb.tile([P, 1], F32, name="eight")
        nc.vector.memset(eight[:], 8.0)

        def load_scale_rows(engine, tile, rows, q):
            engine.dma_start(tile[32 * q : 32 * q + 4, :].bitcast(I32), rows[0, 4 * q : 4 * q + 4, :].bitcast(I32))

        offs_t = load_list(offs, "offs_t")
        ww_raw = sb.tile([P, 2 * H], U8, name="ww_raw")
        nc.scalar.dma_start(ww_raw[:].bitcast(I32), w1_words[0].bitcast(I32))
        n1_t = load_list(n1, "n1_t")
        xw_tab = sb.tile([P, T], U32, name="xw_tab")
        nc.scalar.dma_start(xw_tab[:].bitcast(I32), word_view(x_words))
        for q in range(4):
            load_scale_rows(nc.sync, xs_tab, x_scales, q)
        for q in range(4):
            load_scale_rows(nc.sync if q < 2 else nc.gpsimd, ws_raw, w1_scales, q)
        n2_t = load_list(n2, "n2_t")

        k1_t = load_list(k1, "k1_t")
        dw_tab = sb.tile([P, G], U32, name="dw_tab")
        nc.sync.dma_start(ds_tab[0:P:8, :].bitcast(I32), d_scales[0].bitcast(I32))
        nc.sync.dma_start(dw_tab[:].bitcast(I32), word_view(d_words))
        gain = sb.tile([P, PACK], F32, name="gain")
        nc.sync.dma_start(gain[:], gs.rearrange("(p t) o -> p (t o)", t=PACK))
        n3_t = load_list(n3, "n3_t")
        n4_t = load_list(n4, "n4_t")

        roots = [sb.tile([P, S], F32, name="root%d" % t) for t in range(PACK)]

        warm = sb.tile([P, 1], F32, name="warm")
        nc.scalar.activation(warm[:], eight[:], ACT.Abs_reciprocal_sqrt, bias=eight[:], scale=1.0)

        ww = sb.tile([P, 2 * H], U8, name="ww", align_bytes=64)
        nc.scalar.copy(
            ww[:].bitcast(U16).rearrange("p (t m) -> p t m", t=PACK),
            ww_raw[:].bitcast(U16).rearrange("p (m t) -> p t m", t=PACK),
        )
        xs = sb.tile([P, S], U8, name="xs", align_bytes=64)
        nc.vector.tensor_copy(xs[:], xs_tab[:].indirect(offs_t[:]))
        ws = sb.tile([P, H], U8, name="ws", align_bytes=64)
        ws_dealt = ws[:].rearrange("p (t m) -> p t m", t=PACK)
        ws_given = ws_raw[:].rearrange("p (m t) -> p t m", t=PACK)
        nc.vector.tensor_copy(ws_dealt[:, :1, :], ws_given[:, :1, :])
        nc.vector.tensor_copy(ws_dealt[:, 1:, :], ws_given[:, 1:, :])
        xw = sb.tile([P, S], U32, name="xw", align_bytes=64)
        halves = [slice(u * HALF, (u + 1) * HALF) for u in range(2)]

        def half_of(offsets, u):
            return offsets[:, u * HALF // 16 : (u + 1) * HALF // 16]

        for u in range(2):
            nc.vector.tensor_copy(xw[:, halves[u]], xw_tab[:].indirect(half_of(offs_t, u)))

        def first_product(t, cols, bank):
            y_ps = ps.tile([P, cols.stop - cols.start], F32, name="y_ps%d" % bank, tag="bank%d" % bank)
            nc.tensor.matmul_mx(
                out=y_ps[:],
                lhsT=ww[:, 2 * P * t : 2 * P * (t + 1)].bitcast(FP4X4),
                lhsT_scale=ws[:, P * t : P * (t + 1)],
                rhs=xw[:, cols].bitcast(FP8X4),
                rhs_scale=xs[:, cols],
                start=True,
                stop=True,
            )
            return y_ps

        y = [sb.tile([P, S], F32, name="y%d" % t) for t in range(PACK)]
        for u in range(2):
            nc.scalar.copy(y[0][:, halves[u]], first_product(0, halves[u], PACK * u)[:])
        for t in range(1, PACK):
            nc.vector.tensor_copy(y[t][:], first_product(t, slice(0, S), t)[:])

        larger, smaller, dt = [], [], []

        def fetch_pairs(t):
            pa = sb.tile([P, W], F32, name="pa%d" % t)
            pb = sb.tile([P, W], F32, name="pb%d" % t)
            nc.scalar.activation(pa[:], y[t][:].indirect(n1_t[:]), ACT.Copy)
            nc.scalar.activation(pb[:], y[t][:].indirect(n2_t[:]), ACT.Copy)
            ra = sb.tile([P, W], F32, name="ra%d" % t)
            rb = sb.tile([P, W], F32, name="rb%d" % t)
            nc.vector.tensor_tensor(ra[:], pa[:], pb[:], ALU.max)
            nc.vector.tensor_tensor(rb[:], pa[:], pb[:], ALU.min)
            larger.append(ra)
            smaller.append(rb)
            dt.append(sb.tile([P, S], F32, name="dt%d" % t))

        def put_larger(t):
            nc.scalar.activation(dt[t][:].indirect(n1_t[:]), larger[t][:], ACT.Copy)

        def put_smaller(t):
            nc.scalar.activation(dt[t][:].indirect(n2_t[:]), smaller[t][:], ACT.Copy)
            nc.vector.tensor_scalar(dts[:, t, :], dt[t][:], gain[:, t : t + 1], None, ALU.mult)

        for t in range(PACK):
            fetch_pairs(t)

        dw_g = sb.tile([P, H], U32, name="dw_g", tag="dw_g_then_dts")
        ds_g = sb.tile([P, H], U8, name="ds_g")
        for u in range(2):
            cols = slice(u * H // 2, (u + 1) * H // 2)
            entries = k1_t[:, u * H // 32 : (u + 1) * H // 32]
            nc.vector.tensor_copy(ds_g[:, cols], ds_tab[:].indirect(entries))
        ds_d = sb.tile([P, H], U8, name="ds_d")
        nc.vector.tensor_copy(
            ds_d[:].rearrange("p (t m) -> p t m", t=PACK), ds_g[:].rearrange("p (m t) -> p t m", t=PACK)
        )
        for q in range(4):
            nc.sync.dma_start(
                ds_plane[32 * q : 32 * q + 4, :].bitcast(I32), ds_d[32 * q : 32 * q + 32 : 8, :].bitcast(I32)
            )
        for u in range(2):
            cols = slice(u * H // 2, (u + 1) * H // 2)
            entries = k1_t[:, u * H // 32 : (u + 1) * H // 32]
            nc.vector.tensor_copy(dw_g[:, cols], dw_tab[:].indirect(entries))
        dw = sb.tile([P, H], U32, name="dw", align_bytes=64)
        nc.vector.tensor_copy(
            dw[:].rearrange("p (t m) -> p t m", t=PACK), dw_g[:].rearrange("p (m t) -> p t m", t=PACK)
        )

        dts = sb.tile([P, PACK, S], F32, name="dts", tag="dw_g_then_dts")
        for t0 in (0, 2):
            put_larger(t0)
            put_larger(t0 + 1)
            put_smaller(t0)
            put_smaller(t0 + 1)

        sums = []
        for u in range(2):
            cols = slice(u * HALF, (u + 1) * HALF)
            other = sb.tile([P, PACK, HALF], F32, name="other%d" % u)
            for t in range(PACK):
                nc.scalar.activation(
                    other[:, t, :], dts[:, t, :].indirect(n3_t[:, u * HALF // 16 : (u + 1) * HALF // 16]), ACT.Copy
                )
            z = sb.tile([P, HALF * PACK], BF16, name="z%d" % u, tag="z", align_bytes=64)
            nc.vector.tensor_tensor(
                z[:].rearrange("p (c i t) -> p c t i", i=4, t=PACK),
                dts[:, :, cols].rearrange("p t (c i) -> p c t i", i=4),
                other[:].rearrange("p t (c i) -> p c t i", i=4),
                ALU.subtract,
            )
            zw = sb.tile([P, HALF], U32, name="zw%d" % u, align_bytes=64)
            zs = sb.tile([P, HALF], U8, name="zs%d" % u, align_bytes=64)
            nc.vector.quantize_mx(out=zw[:].bitcast(FP8X4), scales=zs[:], in_=z[:])
            row = []
            for v in range(2):
                h_ps = ps.tile([P, 2, HALF], F32, name="h_ps%d_%d" % (u, v), tag="bank%d" % (PACK + 1 - 5 * u + v))
                for w in range(2):
                    t = 2 * v + w
                    nc.tensor.matmul_mx(
                        out=h_ps[:, w, :],
                        lhsT=dw[:, P * t : P * (t + 1)].bitcast(FP8X4),
                        lhsT_scale=ds_plane[:, P * t : P * (t + 1)],
                        rhs=zw[:].bitcast(FP8X4),
                        rhs_scale=zs[:],
                        start=True,
                        stop=True,
                    )
                row.append(h_ps)
            sums.append(row)

        late_roots = sb.tile([P, PACK - 1, S], F32, name="late_roots")
        for u in range(2):
            size = sb.tile([P, PACK, HALF], F32, name="size%d" % u)
            for v in range(2):
                nc.scalar.activation(size[:, 2 * v : 2 * v + 2, :], sums[u][v][:], ACT.Abs)
            for dst, src in ((roots[0][:, halves[u]], size[:, 0, :]), (late_roots[:, :, halves[u]], size[:, 1:, :])):
                nc.scalar.activation(dst, src, ACT.Abs_reciprocal_sqrt, bias=eight[:], scale=1.0)
        for t in range(1, PACK):
            nc.vector.tensor_tensor(roots[t][:], late_roots[:, t - 1, :], late_roots[:, t - 1, :], ALU.mult)

        out_rows = out.rearrange("(p t) n -> p t n", t=PACK)
        for t in range(PACK):
            fetched = sb.tile([P, S], F32, name="fetched%d" % t)
            result = sb.tile([P, S], F32, name="result%d" % t)
            for u in range(2):
                nc.scalar.activation(fetched[:, halves[u]], roots[t][:].indirect(half_of(n4_t, u)), ACT.Copy)
                nc.vector.tensor_tensor(
                    result[:, halves[u]], sums[u][t // 2][:, t % 2, :], fetched[:, halves[u]], ALU.mult
                )
            if t == 0:
                part = result
                result = sb.tile([P, S], F32, name="result0_whole")
                nc.vector.tensor_tensor(result[:], part[:], fetched[:], ALU.mult)
            nc.sync.dma_start(out_rows[:, t, :], result[:])
